import numpy as np, ml_dtypes
CORES = [36,164,52,180,100,228,116,244]
N = 8
F = 32
BETA, LR = 0.75, 0.5
def setup_inputs(rng):
    return {"gr": rng.standard_normal((N, 128, N * F), dtype=np.float32).astype(ml_dtypes.bfloat16), "m": rng.standard_normal((N, 128, F), dtype=np.float32).astype(ml_dtypes.bfloat16), "w": rng.standard_normal((N, 128, F), dtype=np.float32).astype(ml_dtypes.bfloat16)}
def setup_inputs_big(rng):
    d = setup_inputs(rng)
    for k in ("gr", "m", "w"): d[k] = (d[k].astype(np.float32) * 1048576.0).astype(d[k].dtype)
    return d
def setup_inputs_small(rng):
    d = setup_inputs(rng)
    for k in ("gr", "m", "w"): d[k] = (d[k].astype(np.float32) * (1 / 1048576.0)).astype(d[k].dtype)
    return d
def setup_inputs_apart(rng):
    d = setup_inputs(rng)
    f = (10.0 ** rng.permutation(np.linspace(-1.5, 1.5, N))).astype(np.float32).reshape(N, 1, 1)
    for k in ("gr", "m", "w"): d[k] = (d[k].astype(np.float32) * f).astype(d[k].dtype)
    return d
def reference(gr, m, w):
    GR, M, W = gr.astype(np.float64), m.astype(np.float64), w.astype(np.float64)
    s = GR.sum(axis=0)
    m2 = np.stack([BETA * M[r] + s[:, F * r:F * r + F] for r in range(N)])
    w2 = np.concatenate([W[r] - LR * m2[r] for r in range(N)], axis=1)
    return {"y": np.broadcast_to(w2.astype(ml_dtypes.bfloat16), (N, 128, N * F)), "mo": m2.astype(ml_dtypes.bfloat16)}

@@ -1,0 +1,135 @@
+from concourse.bass import DstId, RemoteDMATransfer
+from concourse.mybir import AluOpType
+
+N, F, P = 8, 32, 128
+Q = P // N
+W = N * F
+BF, FP = "bfloat16", "float32"
+
+SCRATCH = {
+    "stage": ("dram", [N, P, F], BF),
+    "land1": ("dram", [N, P, F], BF),
+    "dsel": ("dram", [N, Q + 1, Q], BF),
+    "esel": ("sbuf", [P, Q + 1], BF),
+    "sel": ("sbuf", [P, Q], BF),
+    "x": ("sbuf", [P, W], BF),
+    "mn": ("sbuf", [P, F], BF),
+    "wn": ("sbuf", [P, F], BF),
+    "t1": ("sbuf", [P, F], BF),
+    "t2": ("sbuf", [P, F], BF),
+    "leaf": ("sbuf", [P, F], BF),
+    "m2": ("sbuf", [P, W], BF),
+    "w2": ("sbuf", [P, W], BF),
+    "m75": ("sbuf", [P, W], BF),
+    "mo2": ("sbuf", [P, W], BF),
+    "h2": ("sbuf", [P, W], BF),
+    "wo2": ("sbuf", [P, W], BF),
+    "c75": ("sbuf", [P, W], BF),
+    "cm05": ("sbuf", [P, W], BF),
+    "yz": ("sbuf", [P, W - F], BF),
+    "yo": ("sbuf", [P, W - F], BF),
+    "ps": ("psum", [P, 512], FP),
+}
+SEMAPHORES = ["es0", "es1", "cst", "staged", "own", "ldn", "ld2", "dselr", "selr", "arr1", "arr2", "sent",
+              "v1", "leafr", "v2", "xr", "mm", "mor", "v3", "wor", "yor", "fin"]
+
+
+def rank_program(g, core, T, topo):
+    r = T.rank_of(core)
+    if r is None:
+        return
+    S = T.sem
+    V, PE, SY, SC = g.vector, g.tensor, g.sync, g.scalar
+    others = [(r + i) % N for i in range(1, N)]
+
+    def blk(t, d):
+        return t[:, F * d:F * (d + 1)]
+
+    def engines(dst):
+        m = topo.mask(core, dst)
+        return [e for e in range(m.bit_length()) if (m >> e) & 1]
+
+    V.memset(T.esel[:, :], 0.0).then_inc(S.es0, 1)
+    V.memset(T.c75[:, :], 0.75).then_inc(S.cst, 1)
+    V.memset(T.cm05[:, :], -0.5).then_inc(S.cst, 1)
+    V.wait_ge(S.es0, 1)
+    V.memset(T.esel[:, 0:1], 1.0).then_inc(S.es1, 1)
+
+    qs = [SY, SC]
+    for i, d in enumerate(others):
+        qs[i % 2].dma_start(T.stage[d], blk(T.gr, d)).then_inc(S.staged, 16)
+    SC.dma_start(T.land1[r], blk(T.gr, r)).then_inc(S.own, 16)
+    SY.dma_start(T.mn[:, :], T.m[:, :]).then_inc(S.ldn, 16)
+    SY.dma_start(T.wn[:, :], T.w[:, :]).then_inc(S.ldn, 16)
+    SC.dma_start(T.m2[0:Q, :], T.m[:, :]).then_inc(S.ld2, 16)
+    SC.dma_start(T.w2[0:Q, :], T.w[:, :]).then_inc(S.ld2, 16)
+    SC.wait_ge(S.es1, 1)
+    SC.dma_start(T.dsel[:, :, :], T.esel[:, :]).then_inc(S.dselr, 16)
+    SC.wait_ge(S.dselr, 16)
+    SC.dma_start(T.sel[:, :], T.dsel[:, 0:Q, :]).then_inc(S.selr, 16)
+
+    g.wait_ge(S.staged, 16 * (N - 1))
+    tr = []
+    for i, d in enumerate(others):
+        dc = T.cores[d]
+        rid, pid = topo.addr(dc, core)
+        tr.append(RemoteDMATransfer(dst_ids=[DstId(rid=rid, pnc=pid)], dma_engine_mask=1 << engines(dc)[i],
+                                    remote_sem=S.arr1, src=T.stage[d], dst=T.land1[r]))
+    g.remote_dma_fused(tr, local_sem=S.sent)
+
+    V.wait_ge(S.cst, 2)
+    V.wait_ge(S.ldn, 32)
+    V.tensor_tensor(out=T.t1[:, :], in0=T.mn[:, :], in1=T.c75[:, 0:F], op=AluOpType.mult).then_inc(S.v1, 1)
+    V.tensor_tensor(out=T.t2[:, :], in0=T.wn[:, :], in1=T.wn[:, :], op=AluOpType.add).then_inc(S.v1, 1)
+    V.wait_ge(S.v1, 2)
+    V.tensor_tensor(out=T.leaf[:, :], in0=T.t1[:, :], in1=T.t2[:, :], op=AluOpType.subtract).then_inc(S.leafr, 1)
+    V.wait_ge(S.ld2, 32)
+    V.tensor_tensor(out=T.m75[0:Q, :], in0=T.m2[0:Q, :], in1=T.c75[0:Q, :], op=AluOpType.mult).then_inc(S.v2, 1)
+
+    g.wait_ge(S.arr1, N - 1)
+    g.wait_ge(S.own, 16)
+    g.wait_ge(S.leafr, 1)
+    ids, dsts, mask = [], [], None
+    for d in others:
+        dc = T.cores[d]
+        rid, pid = topo.addr(dc, core)
+        ids.append(DstId(rid=rid, pnc=pid))
+        k = r if r < d else r - 1
+        dsts.append(T.yz[:, F * k:F * (k + 1)])
+        mask = topo.mask(core, dc) if mask is None else mask & topo.mask(core, dc)
+    ne = len([e for e in range(mask.bit_length()) if (mask >> e) & 1])
+    g.remote_dma_fused([RemoteDMATransfer(dst_ids=ids, dma_engine_mask=mask, remote_sem=S.arr2,
+                                          srcs=[T.land1[j] for j in range(N)] + [T.leaf[:, :]], dsts=dsts, alu_op=1)],
+                       local_sem=S.sent)
+
+    SY.wait_ge(S.arr1, N - 1)
+    SY.wait_ge(S.own, 16)
+    SY.dma_start(T.x[:, :], T.land1[:, :, :]).then_inc(S.xr, 16)
+    PE.wait_ge(S.selr, 16)
+    PE.wait_ge(S.xr, 16)
+    PE.matmul(T.ps[0:Q, 0:W], T.sel[:, :], T.x[:, :], True, True).then_inc(S.mm, 1)
+    V.wait_ge(S.v2, 1)
+    V.wait_ge(S.mm, 1)
+    V.tensor_tensor(out=T.mo2[0:Q, :], in0=T.ps[0:Q, 0:W], in1=T.m75[0:Q, :], op=AluOpType.add).then_inc(S.mor, 1)
+    V.wait_ge(S.mor, 1)
+    V.tensor_tensor(out=T.h2[0:Q, :], in0=T.mo2[0:Q, :], in1=T.cm05[0:Q, :], op=AluOpType.mult).then_inc(S.v3, 1)
+    V.wait_ge(S.v3, 1)
+    V.tensor_tensor(out=T.wo2[0:Q, :], in0=T.w2[0:Q, :], in1=T.h2[0:Q, :], op=AluOpType.add).then_inc(S.wor, 1)
+    SC.wait_ge(S.mor, 1)
+    SC.dma_start(T.mo[:, :], T.mo2[0:Q, :]).then_inc(S.fin, 16)
+    SC.wait_ge(S.wor, 1)
+    SC.dma_start(blk(T.y, r), T.wo2[0:Q, :]).then_inc(S.fin, 16)
+    nfin = 2
+
+    V.wait_ge(S.arr2, ne * (N - 1))
+    V.tensor_tensor(out=T.yo[:, :], in0=T.yz[:, :], in1=T.cm05[:, 0:W - F], op=AluOpType.mult).then_inc(S.yor, 1)
+    if r > 0:
+        SY.wait_ge(S.yor, 1)
+        SY.dma_start(T.y[:, 0:F * r], T.yo[:, 0:F * r]).then_inc(S.fin, 16)
+        nfin += 1
+    if r < N - 1:
+        SC.wait_ge(S.yor, 1)
+        SC.dma_start(T.y[:, F * (r + 1):W], T.yo[:, F * r:W - F]).then_inc(S.fin, 16)
+        nfin += 1
+    g.wait_ge(S.sent, (N - 1) + ne)
+    g.wait_ge(S.fin, 16 * nfin)

@@ -2,36 +2,28 @@ from concourse.bass import DstId, RemoteDMATransfer
 from concourse.mybir import AluOpType
 
 N, F, P = 8, 32, 128
-Q = P // N
 W = N * F
 BF, FP = "bfloat16", "float32"
 
 SCRATCH = {
-    "stage": ("dram", [N, P, F], BF),
-    "land1": ("dram", [N, P, F], BF),
-    "dsel": ("dram", [N, Q + 1, Q], BF),
-    "esel": ("sbuf", [P, Q + 1], BF),
-    "sel": ("sbuf", [P, Q], BF),
-    "x": ("sbuf", [P, W], BF),
+    "gs": ("sbuf", [P, W], BF),
+    "xn": ("sbuf", [P, W], BF),
     "mn": ("sbuf", [P, F], BF),
     "wn": ("sbuf", [P, F], BF),
-    "t1": ("sbuf", [P, F], BF),
-    "t2": ("sbuf", [P, F], BF),
-    "leaf": ("sbuf", [P, F], BF),
-    "m2": ("sbuf", [P, W], BF),
-    "w2": ("sbuf", [P, W], BF),
-    "m75": ("sbuf", [P, W], BF),
-    "mo2": ("sbuf", [P, W], BF),
-    "h2": ("sbuf", [P, W], BF),
-    "wo2": ("sbuf", [P, W], BF),
-    "c75": ("sbuf", [P, W], BF),
-    "cm05": ("sbuf", [P, W], BF),
-    "yz": ("sbuf", [P, W - F], BF),
-    "yo": ("sbuf", [P, W - F], BF),
-    "ps": ("psum", [P, 512], FP),
+    "mh": ("sbuf", [P, P], BF),
+    "nh": ("sbuf", [P, P], BF),
+    "c75": ("sbuf", [P, F], BF),
+    "cm375": ("sbuf", [P, F], BF),
+    "cm2": ("sbuf", [P, F], BF),
+    "a": ("sbuf", [P, F], FP),
+    "tb": ("sbuf", [P, F], FP),
+    "b": ("sbuf", [P, F], FP),
+    "t2": ("sbuf", [P, F], FP),
+    "mos": ("sbuf", [P, F], BF),
+    "yo": ("sbuf", [P, W], BF),
+    "psW": ("psum", [P, 512], FP),
 }
-SEMAPHORES = ["es0", "es1", "cst", "staged", "own", "ldn", "ld2", "dselr", "selr", "arr1", "arr2", "sent",
-              "v1", "leafr", "v2", "xr", "mm", "mor", "v3", "wor", "yor", "fin"]
+SEMAPHORES = ["es0", "es1", "cst", "gsr", "ldn", "v1", "br", "arr1", "mm", "wr", "go", "v2", "mor", "arr2", "sent", "fin"]
 
 
 def rank_program(g, core, T, topo):
@@ -49,87 +41,62 @@ def rank_program(g, core, T, topo):
         m = topo.mask(core, dst)
         return [e for e in range(m.bit_length()) if (m >> e) & 1]
 
-    V.memset(T.esel[:, :], 0.0).then_inc(S.es0, 1)
+    def did(d):
+        rid, pid = topo.addr(T.cores[d], core)
+        return DstId(rid=rid, pnc=pid)
+
+    eng = [e for e in engines(T.cores[others[0]]) if all(e in engines(T.cores[d]) for d in others)]
+    ne = len(eng)
+
+    SY.dma_start(T.gs[:, :], T.gr[:, :]).then_inc(S.gsr, 16)
+    SC.dma_start(T.mn[:, :], T.m[:, :]).then_inc(S.ldn, 16)
+    SC.dma_start(T.wn[:, :], T.w[:, :]).then_inc(S.ldn, 16)
+
+    V.memset(T.mh[:, :], -0.5).then_inc(S.es0, 1)
     V.memset(T.c75[:, :], 0.75).then_inc(S.cst, 1)
-    V.memset(T.cm05[:, :], -0.5).then_inc(S.cst, 1)
-    V.wait_ge(S.es0, 1)
-    V.memset(T.esel[:, 0:1], 1.0).then_inc(S.es1, 1)
+    V.memset(T.cm375[:, :], -0.375).then_inc(S.cst, 1)
+    V.memset(T.cm2[:, :], -2.0).then_inc(S.cst, 1)
+    g.wait_ge(S.es0, 1)
+    g.affine_select(T.nh[:, :], T.mh[:, :], [[-1, P]], AluOpType.is_equal, 0.0, 0, 1).then_inc(S.es1, 1)
 
-    qs = [SY, SC]
-    for i, d in enumerate(others):
-        qs[i % 2].dma_start(T.stage[d], blk(T.gr, d)).then_inc(S.staged, 16)
-    SC.dma_start(T.land1[r], blk(T.gr, r)).then_inc(S.own, 16)
-    SY.dma_start(T.mn[:, :], T.m[:, :]).then_inc(S.ldn, 16)
-    SY.dma_start(T.wn[:, :], T.w[:, :]).then_inc(S.ldn, 16)
-    SC.dma_start(T.m2[0:Q, :], T.m[:, :]).then_inc(S.ld2, 16)
-    SC.dma_start(T.w2[0:Q, :], T.w[:, :]).then_inc(S.ld2, 16)
-    SC.wait_ge(S.es1, 1)
-    SC.dma_start(T.dsel[:, :, :], T.esel[:, :]).then_inc(S.dselr, 16)
-    SC.wait_ge(S.dselr, 16)
-    SC.dma_start(T.sel[:, :], T.dsel[:, 0:Q, :]).then_inc(S.selr, 16)
+    g.wait_ge(S.gsr, 16)
+    g.remote_dma_fused(
+        [RemoteDMATransfer(dst_ids=[did(d)], dma_engine_mask=1 << eng[i], remote_sem=S.arr1, src=blk(T.gs, d), dst=blk(T.xn, r))
+         for i, d in enumerate(others)], local_sem=S.sent)
 
-    g.wait_ge(S.staged, 16 * (N - 1))
-    tr = []
-    for i, d in enumerate(others):
-        dc = T.cores[d]
-        rid, pid = topo.addr(dc, core)
-        tr.append(RemoteDMATransfer(dst_ids=[DstId(rid=rid, pnc=pid)], dma_engine_mask=1 << engines(dc)[i],
-                                    remote_sem=S.arr1, src=T.stage[d], dst=T.land1[r]))
-    g.remote_dma_fused(tr, local_sem=S.sent)
-
-    V.wait_ge(S.cst, 2)
+    V.wait_ge(S.cst, 3)
     V.wait_ge(S.ldn, 32)
-    V.tensor_tensor(out=T.t1[:, :], in0=T.mn[:, :], in1=T.c75[:, 0:F], op=AluOpType.mult).then_inc(S.v1, 1)
-    V.tensor_tensor(out=T.t2[:, :], in0=T.wn[:, :], in1=T.wn[:, :], op=AluOpType.add).then_inc(S.v1, 1)
+    V.tensor_tensor(out=T.a[:, :], in0=T.mn[:, :], in1=T.c75[:, :], op=AluOpType.mult).then_inc(S.v1, 1)
+    V.tensor_tensor(out=T.tb[:, :], in0=T.mn[:, :], in1=T.cm375[:, :], op=AluOpType.mult).then_inc(S.v1, 1)
     V.wait_ge(S.v1, 2)
-    V.tensor_tensor(out=T.leaf[:, :], in0=T.t1[:, :], in1=T.t2[:, :], op=AluOpType.subtract).then_inc(S.leafr, 1)
-    V.wait_ge(S.ld2, 32)
-    V.tensor_tensor(out=T.m75[0:Q, :], in0=T.m2[0:Q, :], in1=T.c75[0:Q, :], op=AluOpType.mult).then_inc(S.v2, 1)
+    V.tensor_tensor(out=T.b[:, :], in0=T.wn[:, :], in1=T.tb[:, :], op=AluOpType.add).then_inc(S.br, 1)
 
-    g.wait_ge(S.arr1, N - 1)
-    g.wait_ge(S.own, 16)
-    g.wait_ge(S.leafr, 1)
-    ids, dsts, mask = [], [], None
-    for d in others:
-        dc = T.cores[d]
-        rid, pid = topo.addr(dc, core)
-        ids.append(DstId(rid=rid, pnc=pid))
-        k = r if r < d else r - 1
-        dsts.append(T.yz[:, F * k:F * (k + 1)])
-        mask = topo.mask(core, dc) if mask is None else mask & topo.mask(core, dc)
-    ne = len([e for e in range(mask.bit_length()) if (mask >> e) & 1])
-    g.remote_dma_fused([RemoteDMATransfer(dst_ids=ids, dma_engine_mask=mask, remote_sem=S.arr2,
-                                          srcs=[T.land1[j] for j in range(N)] + [T.leaf[:, :]], dsts=dsts, alu_op=1)],
-                       local_sem=S.sent)
-
-    SY.wait_ge(S.arr1, N - 1)
-    SY.wait_ge(S.own, 16)
-    SY.dma_start(T.x[:, :], T.land1[:, :, :]).then_inc(S.xr, 16)
-    PE.wait_ge(S.selr, 16)
-    PE.wait_ge(S.xr, 16)
-    PE.matmul(T.ps[0:Q, 0:W], T.sel[:, :], T.x[:, :], True, True).then_inc(S.mm, 1)
-    V.wait_ge(S.v2, 1)
+    PE.wait_ge(S.es1, 1)
+    PE.wait_ge(S.gsr, 16)
+    PE.matmul(T.psW[:, 0:F], T.nh[:, :], blk(T.gs, r), True, False)
+    PE.wait_ge(S.arr1, N - 1)
+    for j in others[:-1]:
+        PE.matmul(T.psW[:, 0:F], T.nh[:, :], blk(T.xn, j), False, False)
+    PE.matmul(T.psW[:, 0:F], T.nh[:, :], blk(T.xn, others[-1]), False, True).then_inc(S.mm, 1)
+    V.wait_ge(S.br, 1)
     V.wait_ge(S.mm, 1)
-    V.tensor_tensor(out=T.mo2[0:Q, :], in0=T.ps[0:Q, 0:W], in1=T.m75[0:Q, :], op=AluOpType.add).then_inc(S.mor, 1)
-    V.wait_ge(S.mor, 1)
-    V.tensor_tensor(out=T.h2[0:Q, :], in0=T.mo2[0:Q, :], in1=T.cm05[0:Q, :], op=AluOpType.mult).then_inc(S.v3, 1)
-    V.wait_ge(S.v3, 1)
-    V.tensor_tensor(out=T.wo2[0:Q, :], in0=T.w2[0:Q, :], in1=T.h2[0:Q, :], op=AluOpType.add).then_inc(S.wor, 1)
-    SC.wait_ge(S.mor, 1)
-    SC.dma_start(T.mo[:, :], T.mo2[0:Q, :]).then_inc(S.fin, 16)
-    SC.wait_ge(S.wor, 1)
-    SC.dma_start(blk(T.y, r), T.wo2[0:Q, :]).then_inc(S.fin, 16)
-    nfin = 2
+    V.tensor_tensor(out=blk(T.yo, r), in0=T.psW[:, 0:F], in1=T.b[:, :], op=AluOpType.add).then_inc(S.wr, 1)
 
-    V.wait_ge(S.arr2, ne * (N - 1))
-    V.tensor_tensor(out=T.yo[:, :], in0=T.yz[:, :], in1=T.cm05[:, 0:W - F], op=AluOpType.mult).then_inc(S.yor, 1)
-    if r > 0:
-        SY.wait_ge(S.yor, 1)
-        SY.dma_start(T.y[:, 0:F * r], T.yo[:, 0:F * r]).then_inc(S.fin, 16)
-        nfin += 1
-    if r < N - 1:
-        SC.wait_ge(S.yor, 1)
-        SC.dma_start(T.y[:, F * (r + 1):W], T.yo[:, F * r:W - F]).then_inc(S.fin, 16)
-        nfin += 1
+    g.wait_ge(S.wr, 1)
+    g.remote_dma_fused(
+        [RemoteDMATransfer(dst_ids=[did(d) for d in others], dma_engine_mask=sum(1 << e for e in eng), remote_sem=S.arr2,
+                           srcs=[blk(T.yo, r)], dsts=[blk(T.yo, r) for d in others])], local_sem=S.sent)
+    g.sem_inc(S.go, 1)
+
+    V.tensor_tensor(out=T.t2[:, :], in0=T.psW[:, 0:F], in1=T.cm2[:, :], op=AluOpType.mult).then_inc(S.v2, 1)
+    V.wait_ge(S.v2, 1)
+    V.tensor_tensor(out=T.mos[:, :], in0=T.t2[:, :], in1=T.a[:, :], op=AluOpType.add).then_inc(S.mor, 1)
+    SC.wait_ge(S.mor, 1)
+    SC.wait_ge(S.go, 1)
+    SC.dma_start(T.mo[:, :], T.mos[:, :]).then_inc(S.fin, 16)
+
+    SY.wait_ge(S.wr, 1)
+    SY.wait_ge(S.arr2, ne * (N - 1))
+    SY.dma_start(T.y[:, :], T.yo[:, :]).then_inc(S.fin, 16)
     g.wait_ge(S.sent, (N - 1) + ne)
-    g.wait_ge(S.fin, 16 * nfin)
+    g.wait_ge(S.fin, 32)

from concourse.bass import DstId, RemoteDMATransfer
from concourse.mybir import AluOpType

N, F, P = 8, 32, 128
W = N * F
BF, FP = "bfloat16", "float32"

SCRATCH = {
    "gs": ("sbuf", [P, W], BF),
    "xn": ("sbuf", [P, W], BF),
    "mn": ("sbuf", [P, F], BF),
    "wn": ("sbuf", [P, F], BF),
    "mh": ("sbuf", [P, P], BF),
    "nh": ("sbuf", [P, P], BF),
    "c75": ("sbuf", [P, F], BF),
    "cm375": ("sbuf", [P, F], BF),
    "cm2": ("sbuf", [P, F], BF),
    "a": ("sbuf", [P, F], FP),
    "tb": ("sbuf", [P, F], FP),
    "b": ("sbuf", [P, F], FP),
    "t2": ("sbuf", [P, F], FP),
    "mos": ("sbuf", [P, F], BF),
    "yo": ("sbuf", [P, W], BF),
    "psW": ("psum", [P, 512], FP),
}
SEMAPHORES = ["es0", "es1", "cst", "gsr", "ldn", "v1", "br", "arr1", "mm", "wr", "go", "v2", "mor", "arr2", "sent", "fin"]


def rank_program(g, core, T, topo):
    r = T.rank_of(core)
    if r is None:
        return
    S = T.sem
    V, PE, SY, SC = g.vector, g.tensor, g.sync, g.scalar
    others = [(r + i) % N for i in range(1, N)]

    def blk(t, d):
        return t[:, F * d:F * (d + 1)]

    def engines(dst):
        m = topo.mask(core, dst)
        return [e for e in range(m.bit_length()) if (m >> e) & 1]

    def did(d):
        rid, pid = topo.addr(T.cores[d], core)
        return DstId(rid=rid, pnc=pid)

    eng = [e for e in engines(T.cores[others[0]]) if all(e in engines(T.cores[d]) for d in others)]
    ne = len(eng)

    SY.dma_start(T.gs[:, :], T.gr[:, :]).then_inc(S.gsr, 16)
    SC.dma_start(T.mn[:, :], T.m[:, :]).then_inc(S.ldn, 16)
    SC.dma_start(T.wn[:, :], T.w[:, :]).then_inc(S.ldn, 16)

    V.memset(T.mh[:, :], -0.5).then_inc(S.es0, 1)
    V.memset(T.c75[:, :], 0.75).then_inc(S.cst, 1)
    V.memset(T.cm375[:, :], -0.375).then_inc(S.cst, 1)
    V.memset(T.cm2[:, :], -2.0).then_inc(S.cst, 1)
    g.wait_ge(S.es0, 1)
    g.affine_select(T.nh[:, :], T.mh[:, :], [[-1, P]], AluOpType.is_equal, 0.0, 0, 1).then_inc(S.es1, 1)

    g.wait_ge(S.gsr, 16)
    g.remote_dma_fused(
        [RemoteDMATransfer(dst_ids=[did(d)], dma_engine_mask=1 << eng[i], remote_sem=S.arr1, src=blk(T.gs, d), dst=blk(T.xn, r))
         for i, d in enumerate(others)], local_sem=S.sent)

    V.wait_ge(S.cst, 3)
    V.wait_ge(S.ldn, 32)
    V.tensor_tensor(out=T.a[:, :], in0=T.mn[:, :], in1=T.c75[:, :], op=AluOpType.mult).then_inc(S.v1, 1)
    V.tensor_tensor(out=T.tb[:, :], in0=T.mn[:, :], in1=T.cm375[:, :], op=AluOpType.mult).then_inc(S.v1, 1)
    V.wait_ge(S.v1, 2)
    V.tensor_tensor(out=T.b[:, :], in0=T.wn[:, :], in1=T.tb[:, :], op=AluOpType.add).then_inc(S.br, 1)

    PE.wait_ge(S.es1, 1)
    PE.wait_ge(S.gsr, 16)
    PE.matmul(T.psW[:, 0:F], T.nh[:, :], blk(T.gs, r), True, False)
    PE.wait_ge(S.arr1, N - 1)
    for j in others[:-1]:
        PE.matmul(T.psW[:, 0:F], T.nh[:, :], blk(T.xn, j), False, False)
    PE.matmul(T.psW[:, 0:F], T.nh[:, :], blk(T.xn, others[-1]), False, True).then_inc(S.mm, 1)
    V.wait_ge(S.br, 1)
    V.wait_ge(S.mm, 1)
    V.tensor_tensor(out=blk(T.yo, r), in0=T.psW[:, 0:F], in1=T.b[:, :], op=AluOpType.add).then_inc(S.wr, 1)

    g.wait_ge(S.wr, 1)
    g.remote_dma_fused(
        [RemoteDMATransfer(dst_ids=[did(d) for d in others], dma_engine_mask=sum(1 << e for e in eng), remote_sem=S.arr2,
                           srcs=[blk(T.yo, r)], dsts=[blk(T.yo, r) for d in others])], local_sem=S.sent)
    g.sem_inc(S.go, 1)

    V.tensor_tensor(out=T.t2[:, :], in0=T.psW[:, 0:F], in1=T.cm2[:, :], op=AluOpType.mult).then_inc(S.v2, 1)
    V.wait_ge(S.v2, 1)
    V.tensor_tensor(out=T.mos[:, :], in0=T.t2[:, :], in1=T.a[:, :], op=AluOpType.add).then_inc(S.mor, 1)
    SC.wait_ge(S.mor, 1)
    SC.wait_ge(S.go, 1)
    SC.dma_start(T.mo[:, :], T.mos[:, :]).then_inc(S.fin, 16)

    SY.wait_ge(S.wr, 1)
    SY.wait_ge(S.arr2, ne * (N - 1))
    SY.dma_start(T.y[:, :], T.yo[:, :]).then_inc(S.fin, 16)
    g.wait_ge(S.sent, (N - 1) + ne)
    g.wait_ge(S.fin, 32)
